import numpy as np
import ml_dtypes


def mxq(x, axis, fmt="e4m3"):
    dtype, down = {"e4m3": (ml_dtypes.float8_e4m3fn, 7), "e5m2": (ml_dtypes.float8_e5m2, 14)}[fmt]
    v = np.moveaxis(np.asarray(x, np.float32).astype(ml_dtypes.bfloat16).astype(np.float64), axis, -1)
    blocks = v.reshape(v.shape[:-1] + (-1, 32))
    amax = np.abs(blocks).max(-1, keepdims=True)
    byte = np.maximum(np.where(amax > 0, np.frexp(amax)[1] - 1 + 127, 0) - down, 1)
    scale = np.exp2(byte - 127.0)
    codes = (blocks / scale).astype(np.float32).astype(dtype).astype(np.float64)
    return np.moveaxis((codes * scale).reshape(v.shape), -1, axis)


WIDE = False


def mx_kscale(k):
    if not WIDE:
        return np.ones(k)
    levels = np.array([18, -18])
    if k % 512:
        return np.exp2(np.random.permutation(np.resize(levels, k // 32))).repeat(32)
    a = np.empty((k // 512, 16))
    for p in range(k // 512):
        a[p, :8] = np.random.permutation(np.resize(levels, 8))
        for g in range(8):
            far = levels[np.abs(levels - a[p, g]) >= 10]
            a[p, g + 8] = far[np.random.randint(len(far))]
    return np.exp2(a.ravel()).repeat(32)


def f64(x):
    return np.asarray(x).astype(np.float64)


def striped(idx):
    return np.tile(np.asarray(idx).reshape(-1, 16).T, (8, 1)).astype(np.uint16)


def unstriped(offs):
    return offs[:16].T.reshape(-1).astype(np.int64)


def sig(x):
    return 1.0 / (1.0 + np.exp(-x))


def setup_inputs():
    n = np.random.standard_normal
    uni = np.random.uniform
    order = np.random.permutation(2048)
    idx = order[:512]
    jdx = order[512:1024]
    soft_kp = np.exp(n((512, 512)))
    f_d = mx_kscale(512)
    f_r = mx_kscale(512)
    return {
        "xT": (0.35 * n((512, 512)) * f_d[:, None] * f_r[None, :]).astype(np.float32),
        "wT": (n((512, 2048)) / np.sqrt(512) / f_d[:, None]).astype(np.float32),
        "us": (uni(0.75, 1.3, (512, 1)) / f_r[:, None]).astype(np.float32),
        "ts": np.tile(uni(0.75, 1.3, 2048), (128, 1)).astype(np.float32),
        "y": (np.random.randint(0, 2, (512, 512))).astype(np.float32),
        "kp": (soft_kp / soft_kp.sum(-1, keepdims=True)).astype(np.float32),
        "w1": (uni(0.75, 1.3, (512, 1))).astype(np.float32),
        "w2": (uni(150.0, 250.0, (512, 1))).astype(np.float32),
        "offs": striped(idx),
        "joffs": striped(jdx),
    }


def reference(xT, wT, us, ts, y, kp, w1, w2, offs, joffs):
    idx = unstriped(offs)
    jdx = unstriped(joffs)
    wn = f64(wT)[:, idx]
    wo = f64(wT)[:, jdx]
    ts_i = f64(ts)[:1][:, idx]
    ts_j = f64(ts)[:1][:, jdx]
    q_xT = mxq(f64(xT), 0, "e4m3")
    a = q_xT.T @ mxq(wn, 0, "e4m3")
    b = q_xT.T @ mxq(wo, 0, "e4m3")
    g = f64(w1) * f64(us) * ts_i * (sig(f64(us) * ts_i * a) - f64(y))
    z = f64(us) * ts_j * b
    m = (z).max(-1, keepdims=True)
    e = np.exp(z - m)
    tot = (e).sum(-1, keepdims=True)
    h = f64(w2) * f64(us) * ts_j * (e / tot - f64(kp))
    q_xT_2 = mxq(f64(xT), 1, "e4m3")
    d1 = q_xT_2 @ mxq(g, 0, "e5m2")
    d2 = q_xT_2 @ mxq(h, 0, "e5m2")
    pa = np.zeros((512, 2048))
    pa[:, idx] = d1
    pb = np.zeros((512, 2048))
    pb[:, jdx] = d2
    out = pa + pb
    return out

@@ -1,0 +1,275 @@
+from contextlib import ExitStack
+
+import concourse.mybir as mybir
+from concourse.masks import make_identity
+
+D, R, N, T = 512, 512, 512, 2048
+FLOPS = 4 * 2 * D * R * N
+
+F32 = mybir.dt.float32
+BF16 = mybir.dt.bfloat16
+U32 = mybir.dt.uint32
+U16 = mybir.dt.uint16
+U8 = mybir.dt.uint8
+E4M3 = mybir.dt.float8_e4m3fn_x4
+E5M2 = mybir.dt.float8_e5m2_x4
+ALU = mybir.AluOpType
+ACT = mybir.ActivationFunctionType
+AX = mybir.AxisListType
+
+P = 128
+PACK = 4
+W_CHUNK = 512
+
+
+def tile_attend_glwf_kernel(tc, xT, wT, us, ts, y, kp, w1, w2, offs, joffs, out):
+    nc = tc.nc
+    with ExitStack() as ctx:
+        sb = ctx.enter_context(tc.tile_pool(name="sb", bufs=1))
+        ps = ctx.enter_context(tc.psum_pool(name="ps", bufs=1))
+        bank = [ps.tile([P, N], F32, name="bank%d" % b) for b in range(8)]
+
+        def quantize(name, src, fmt):
+            codes = sb.tile([P, N], U32, name=name + "_codes", align_bytes=64)
+            scales = sb.tile([P, N], U8, name=name + "_scales", align_bytes=64)
+            nc.vector.quantize_mx(out=codes[:].bitcast(fmt), scales=scales[:], in_=src[:])
+            return codes, scales, fmt
+
+        def product(dst, stat, block, mov):
+            cols = slice(block * P, (block + 1) * P)
+            nc.tensor.matmul_mx(
+                out=dst[:],
+                lhsT=stat[0][:, cols].bitcast(stat[2]),
+                lhsT_scale=stat[1][:, cols],
+                rhs=mov[0][:].bitcast(mov[2]),
+                rhs_scale=mov[1][:],
+                start=True,
+                stop=True,
+            )
+
+        new_list = sb.tile([P, N // 16], U16, name="new_list")
+        old_list = sb.tile([P, N // 16], U16, name="old_list")
+        x_raw = sb.tile([P, PACK, R], F32, name="x_raw", tag="x_raw")
+        nc.sync.dma_start(out=x_raw[:], in_=xT.rearrange("(p t) r -> p t r", t=PACK))
+        nc.sync.dma_start(new_list[:], offs)
+        nc.sync.dma_start(old_list[:], joffs)
+
+        ts_window = sb.tile([P, T], F32, name="ts_window", tag="ts_window")
+        nc.vector.memset(ts_window[:], 0.0)
+        nc.scalar.dma_start(out=ts_window[0:1, :], in_=ts[0:1, :])
+
+        row_vec = {}
+        for name, src in (("us", us), ("w1", w1), ("w2", w2)):
+            row_vec[name] = sb.tile([P, PACK], F32, name=name + "_rows")
+            nc.gpsimd.dma_start(out=row_vec[name][:], in_=src.rearrange("(p j) o -> p (j o)", j=PACK))
+
+        w_rows = wT.rearrange("(p t) c -> p t c", t=PACK)
+        w_raw = []
+        for u in range(2):
+            for c0 in range(0, T, W_CHUNK):
+                raw = sb.tile([P, 2, W_CHUNK], F32, name="w_raw%d_%d" % (u, c0))
+                nc.sync.dma_start(out=raw[:], in_=w_rows[:, 2 * u : 2 * u + 2, c0 : c0 + W_CHUNK])
+                w_raw.append((u, c0, raw))
+
+        y_rows = y.rearrange("(p j) i -> p j i", j=PACK)
+        y_sb = []
+        for j in range(PACK):
+            y_j = sb.tile([P, N], F32, name="y%d" % j)
+            nc.sync.dma_start(out=y_j[:], in_=y_rows[:, j, :])
+            y_sb.append(y_j)
+        kp_sb = sb.tile([P, PACK, N], F32, name="kp_sb")
+        nc.sync.dma_start(out=kp_sb[:], in_=kp.rearrange("(p j) i -> p j i", j=PACK))
+
+        ident = sb.tile([P, P], F32, name="ident")
+        make_identity(nc, ident[:])
+
+        table_warm = sb.tile([P, 1], F32, name="table_warm")
+        nc.scalar.activation(out=table_warm[:], in_=ident[:, 0:1], func=ACT.Exp)
+
+        window = []
+        for t in range(2):
+            win = sb.tile([P, T], F32, name="window%d" % t)
+            nc.vector.memset(win[:], 0.0)
+            window.append(win)
+
+        x_by_d = sb.tile([P, PACK * R], BF16, name="x_by_d", align_bytes=64)
+        nc.vector.tensor_copy(
+            out=x_by_d[:].rearrange("p (j s t) -> p j s t", j=PACK, t=PACK),
+            in_=x_raw[:].rearrange("p t (s j) -> p j s t", j=PACK),
+        )
+
+        window.append(sb.tile([P, T], F32, name="window2", tag="x_raw"))
+        nc.gpsimd.memset(window[2][:], 0.0)
+
+        ts_col = []
+        ts_row = []
+        for k, lst in enumerate((new_list, old_list)):
+            picked = sb.tile([P, N], F32, name="ts_picked%d" % k)
+            nc.vector.tensor_copy(out=picked[:], in_=ts_window[:].indirect(lst[:]))
+            for q in range(PACK):
+                cols = slice(q * P, (q + 1) * P)
+                nc.tensor.transpose(bank[k][:, cols], picked[:, cols], ident[:])
+            col = sb.tile([P, PACK], F32, name="ts_col%d" % k)
+            nc.scalar.copy(out=col[:], in_=bank[k][:, 0:N:P])
+            for q in range(PACK):
+                cols = slice(q * P, (q + 1) * P)
+                nc.tensor.transpose(bank[2 + k][:, cols], col[:, q : q + 1].to_broadcast([P, P]), ident[:])
+            row = sb.tile([P, N], F32, name="ts_row%d" % k)
+            nc.scalar.copy(out=row[:], in_=bank[2 + k][:])
+            ts_col.append(col)
+            ts_row.append(row)
+
+        xq_d = quantize("xq_d", x_by_d, E4M3)
+        window.append(sb.tile([P, T], F32, name="window3", tag="ts_window"))
+        nc.gpsimd.memset(window[3][:], 0.0)
+
+        us_half = sb.tile([P, PACK], F32, name="us_half")
+        c1_half = sb.tile([P, PACK], F32, name="c1_half")
+        c1_neg = sb.tile([P, PACK], F32, name="c1_neg")
+        c2 = sb.tile([P, PACK], F32, name="c2")
+        c2_neg = sb.tile([P, PACK], F32, name="c2_neg")
+        minus_one = sb.tile([P, PACK], F32, name="minus_one")
+        nc.gpsimd.memset(minus_one[:], -1.0)
+        nc.gpsimd.tensor_scalar(us_half[:], row_vec["us"][:], 0.5, 0.0, ALU.mult, ALU.add)
+        nc.gpsimd.tensor_tensor(c1_half[:], row_vec["w1"][:], us_half[:], ALU.mult)
+        nc.gpsimd.tensor_scalar(c1_neg[:], c1_half[:], -2.0, 0.0, ALU.mult, ALU.add)
+        nc.gpsimd.tensor_tensor(c2[:], row_vec["w2"][:], row_vec["us"][:], ALU.mult)
+        nc.gpsimd.tensor_scalar(c2_neg[:], c2[:], -1.0, 0.0, ALU.mult, ALU.add)
+
+        x_words = x_by_d[:].bitcast(F32).rearrange("p (j s u) -> p j s u", j=PACK, u=2)
+        for u in range(2):
+            for j in range(PACK):
+                nc.tensor.transpose(bank[2 + u][:, j * P : (j + 1) * P], x_words[:, j, :, u], ident[:])
+
+        w_pairs = [sb.tile([P, 2 * T], BF16, name="w_pairs%d" % u) for u in range(2)]
+        w_new = sb.tile([P, PACK * N], BF16, name="w_new", align_bytes=64)
+        w_old = sb.tile([P, PACK * N], BF16, name="w_old", align_bytes=64)
+        old_halves = sb.tile([P, 2, N], U32, name="old_halves")
+        new_words = w_new[:].bitcast(U32).rearrange("p (c u) -> p c u", u=2)
+        for u, c0, raw in w_raw:
+            dst = w_pairs[u][:, 2 * c0 : 2 * (c0 + W_CHUNK)].rearrange("p (c e) -> p c e", e=2)
+            src = raw[:].rearrange("p e c -> p c e")
+            if u == 1 and c0 + W_CHUNK == T:
+                nc.vector.tensor_copy(out=dst, in_=src)
+            else:
+                nc.scalar.activation(out=dst, in_=src, func=ACT.Copy)
+            if c0 + W_CHUNK == T:
+                words = w_pairs[u][:].bitcast(U32)
+                nc.vector.tensor_copy(out=new_words[:, :, u], in_=words.indirect(new_list[:]))
+                if u == 1:
+                    wq_new = quantize("wq_new", w_new, E4M3)
+                nc.vector.tensor_copy(out=old_halves[:, u, :], in_=words.indirect(old_list[:]))
+        nc.scalar.copy(
+            out=w_old[:].bitcast(U32).rearrange("p (c u) -> p c u", u=2),
+            in_=old_halves[:].rearrange("p u c -> p c u"),
+        )
+
+        x_by_r = sb.tile([P, PACK * D], BF16, name="x_by_r", align_bytes=64)
+        for u in range(2):
+            nc.scalar.copy(
+                out=x_by_r[:, u * 2 * D : (u + 1) * 2 * D].rearrange("s (e p j) -> s e p j", e=2, j=PACK),
+                in_=bank[2 + u][:].bitcast(BF16).rearrange("s (j p e) -> s e p j", j=PACK, e=2),
+            )
+
+        def add_turned(banks, src, j, first, last):
+            for q in range(PACK):
+                nc.tensor.matmul(
+                    banks[q][:, j * P : (j + 1) * P],
+                    src[:, q * P : (q + 1) * P],
+                    ident[:],
+                    start=first,
+                    stop=last,
+                    is_transpose=True,
+                )
+
+        def finish_gradient(name, banks, col):
+            by_slot = sb.tile([P, PACK, R], BF16, name=name + "_by_slot")
+            grad = sb.tile([P, PACK * N], BF16, name=name + "_by_r", align_bytes=64)
+            grad_words = grad[:].bitcast(F32)
+            for q in range(PACK):
+                nc.scalar.activation(
+                    out=by_slot[:, q, :].rearrange("p (s j) -> p s j", j=PACK),
+                    in_=banks[q][:].rearrange("p (j s) -> p s j", j=PACK),
+                    func=ACT.Copy,
+                    scale=col[:, q : q + 1],
+                )
+                if q % 2 == 1:
+                    back = banks[q // 2]
+                    for qq in (q - 1, q):
+                        words = by_slot[:, qq, :].bitcast(F32).rearrange("p (s u) -> p s u", u=2)
+                        for u in range(2):
+                            place = 2 * (qq % 2) + u
+                            nc.tensor.transpose(back[:, place * P : (place + 1) * P], words[:, :, u], ident[:])
+            for half in range(2):
+                nc.scalar.copy(
+                    out=grad_words[:, half * N : (half + 1) * N].rearrange("s (q p u) -> s q p u", q=2, u=2),
+                    in_=banks[half][:].rearrange("s (q u p) -> s q p u", q=2, u=2),
+                )
+            return quantize(name, grad, E5M2)
+
+        g_banks = bank[4:8]
+        for j in range(PACK):
+            nc.gpsimd.tensor_scalar(
+                y_sb[j][:], y_sb[j][:], c1_neg[:, j : j + 1], c1_half[:, j : j + 1], ALU.mult, ALU.add
+            )
+            add_turned(g_banks, y_sb[j], j, j == 0, False)
+        act = []
+        for j in range(PACK):
+            product(bank[j % 2], xq_d, j, wq_new)
+            a_j = sb.tile([P, N], F32, name="a%d" % j)
+            nc.vector.tensor_tensor(a_j[:], bank[j % 2][:], ts_row[0][:], ALU.mult)
+            nc.scalar.activation(out=a_j[:], in_=a_j[:], func=ACT.Tanh, scale=us_half[:, j : j + 1])
+            act.append(a_j)
+        wq_old = quantize("wq_old", w_old, E4M3)
+        for j in range(PACK):
+            nc.vector.tensor_scalar(act[j][:], act[j][:], c1_half[:, j : j + 1], None, ALU.mult)
+            add_turned(g_banks, act[j], j, False, j == PACK - 1)
+        xq_r = quantize("xq_r", x_by_r, E4M3)
+        gq = finish_gradient("g", g_banks, ts_col[0])
+
+        z = []
+        neg_max = sb.tile([P, PACK], F32, name="neg_max")
+        for j in range(PACK):
+            b_bank = bank[(j + 2) % 4]
+            product(b_bank, xq_d, j, wq_old)
+            z_j = sb.tile([P, N], F32, name="z%d" % j)
+            nc.vector.scalar_tensor_tensor(
+                z_j[:], b_bank[:], row_vec["us"][:, j : j + 1], ts_row[1][:], ALU.mult, ALU.mult
+            )
+            z.append(z_j)
+        for j in range(PACK):
+            nc.vector.tensor_reduce(neg_max[:, j : j + 1], z[j][:], AX.X, ALU.max, negate=True)
+
+        def place(name, grad_q, lst, t):
+            acc = bank[4 + (t + 2) % 4]
+            product(acc, xq_r, t, grad_q)
+            staged = sb.tile([P, N], F32, name="%s_staged%d" % (name, t))
+            nc.scalar.copy(out=staged[:], in_=acc[:])
+            nc.vector.tensor_copy(out=window[t][:].indirect(lst[:]), in_=staged[:])
+
+        for t in range(PACK):
+            place("d1", gq, new_list, t)
+
+        h_banks = bank[0:4]
+        total = sb.tile([P, PACK], F32, name="total")
+        e_scale = sb.tile([P, PACK], F32, name="e_scale")
+        for j in range(PACK):
+            nc.scalar.activation(
+                out=z[j][:], in_=z[j][:], func=ACT.Exp, bias=neg_max[:, j : j + 1], accum_out=total[:, j : j + 1]
+            )
+        for j in range(PACK):
+            nc.gpsimd.tensor_scalar(
+                kp_sb[:, j, :], kp_sb[:, j, :], c2_neg[:, j : j + 1], 0.0, ALU.mult, ALU.add
+            )
+            add_turned(h_banks, kp_sb[:, j, :], j, j == 0, False)
+        nc.gpsimd.tensor_tensor(total[:], total[:], minus_one[:], ALU.pow)
+        nc.gpsimd.tensor_tensor(e_scale[:], total[:], c2[:], ALU.mult)
+        for j in range(PACK):
+            nc.scalar.activation(out=z[j][:], in_=z[j][:], func=ACT.Copy, scale=e_scale[:, j : j + 1])
+            add_turned(h_banks, z[j], j, False, j == PACK - 1)
+        hq = finish_gradient("h", h_banks, ts_col[1])
+
+        out_rows = out.rearrange("(p t) c -> p t c", t=PACK)
+        for t in range(PACK):
+            place("d2", hq, old_list, t)
+            nc.sync.dma_start(out=out_rows[:, t, :], in_=window[t][:])

@@ -30,7 +30,7 @@ def tile_attend_glwf_kernel(tc, xT, wT, us, ts, y, kp, w1, w2, offs, joffs, out)
         bank = [ps.tile([P, N], F32, name="bank%d" % b) for b in range(8)]
 
         def quantize(name, src, fmt):
-            codes = sb.tile([P, N], U32, name=name + "_codes", align_bytes=64)
+            codes = sb.tile([P, N], U32, name=name + "_codes", tag=name + "_codes", align_bytes=64)
             scales = sb.tile([P, N], U8, name=name + "_scales", align_bytes=64)
             nc.vector.quantize_mx(out=codes[:].bitcast(fmt), scales=scales[:], in_=src[:])
             return codes, scales, fmt
@@ -47,29 +47,33 @@ def tile_attend_glwf_kernel(tc, xT, wT, us, ts, y, kp, w1, w2, offs, joffs, out)
                 stop=True,
             )
 
+        ident = sb.tile([P, P], F32, name="ident")
+        make_identity(nc, ident[:])
+
         new_list = sb.tile([P, N // 16], U16, name="new_list")
         old_list = sb.tile([P, N // 16], U16, name="old_list")
-        x_raw = sb.tile([P, PACK, R], F32, name="x_raw", tag="x_raw")
+        x_raw = sb.tile([P, PACK, R], F32, name="x_raw", tag="x_raw", align_bytes=64)
         nc.sync.dma_start(out=x_raw[:], in_=xT.rearrange("(p t) r -> p t r", t=PACK))
         nc.sync.dma_start(new_list[:], offs)
         nc.sync.dma_start(old_list[:], joffs)
 
-        ts_window = sb.tile([P, T], F32, name="ts_window", tag="ts_window")
-        nc.vector.memset(ts_window[:], 0.0)
-        nc.scalar.dma_start(out=ts_window[0:1, :], in_=ts[0:1, :])
-
-        row_vec = {}
-        for name, src in (("us", us), ("w1", w1), ("w2", w2)):
-            row_vec[name] = sb.tile([P, PACK], F32, name=name + "_rows")
-            nc.gpsimd.dma_start(out=row_vec[name][:], in_=src.rearrange("(p j) o -> p (j o)", j=PACK))
+        ts_window = sb.tile([P, T], F32, name="ts_window", tag="ts_window", align_bytes=64)
+        nc.sync.dma_start(out=ts_window[0:32, :], in_=ts[0:32, :])
+        nc.gpsimd.memset(ts_window[32:64, :], 0.0)
+        nc.vector.memset(ts_window[64:128, :], 0.0)
 
         w_rows = wT.rearrange("(p t) c -> p t c", t=PACK)
         w_raw = []
         for u in range(2):
             for c0 in range(0, T, W_CHUNK):
-                raw = sb.tile([P, 2, W_CHUNK], F32, name="w_raw%d_%d" % (u, c0))
+                raw = sb.tile([P, 2, W_CHUNK], F32, name="w_raw%d_%d" % (u, c0), tag="w_raw%d_%d" % (u, c0), align_bytes=64)
                 nc.sync.dma_start(out=raw[:], in_=w_rows[:, 2 * u : 2 * u + 2, c0 : c0 + W_CHUNK])
                 w_raw.append((u, c0, raw))
+
+        row_vec = {}
+        for name, src in (("us", us), ("w1", w1), ("w2", w2)):
+            row_vec[name] = sb.tile([P, PACK], F32, name=name + "_rows")
+            nc.sync.dma_start(out=row_vec[name][:], in_=src.rearrange("(p j) o -> p (j o)", j=PACK))
 
         y_rows = y.rearrange("(p j) i -> p j i", j=PACK)
         y_sb = []
@@ -80,17 +84,17 @@ def tile_attend_glwf_kernel(tc, xT, wT, us, ts, y, kp, w1, w2, offs, joffs, out)
         kp_sb = sb.tile([P, PACK, N], F32, name="kp_sb")
         nc.sync.dma_start(out=kp_sb[:], in_=kp.rearrange("(p j) i -> p j i", j=PACK))
 
-        ident = sb.tile([P, P], F32, name="ident")
-        make_identity(nc, ident[:])
-
         table_warm = sb.tile([P, 1], F32, name="table_warm")
         nc.scalar.activation(out=table_warm[:], in_=ident[:, 0:1], func=ACT.Exp)
 
-        window = []
-        for t in range(2):
-            win = sb.tile([P, T], F32, name="window%d" % t)
-            nc.vector.memset(win[:], 0.0)
-            window.append(win)
+        window = {}
+
+        def clear_window(t, slot):
+            window[t] = sb.tile([P, T], F32, name="window%d" % t, tag=slot, align_bytes=64)
+            nc.gpsimd.memset(window[t][:], 0.0)
+
+        window[2] = sb.tile([P, T], F32, name="window2")
+        nc.vector.memset(window[2][:], 0.0)
 
         x_by_d = sb.tile([P, PACK * R], BF16, name="x_by_d", align_bytes=64)
         nc.vector.tensor_copy(
@@ -98,8 +102,7 @@ def tile_attend_glwf_kernel(tc, xT, wT, us, ts, y, kp, w1, w2, offs, joffs, out)
             in_=x_raw[:].rearrange("p t (s j) -> p j s t", j=PACK),
         )
 
-        window.append(sb.tile([P, T], F32, name="window2", tag="x_raw"))
-        nc.gpsimd.memset(window[2][:], 0.0)
+        clear_window(1, "x_raw")
 
         ts_col = []
         ts_row = []
@@ -110,18 +113,14 @@ def tile_attend_glwf_kernel(tc, xT, wT, us, ts, y, kp, w1, w2, offs, joffs, out)
                 cols = slice(q * P, (q + 1) * P)
                 nc.tensor.transpose(bank[k][:, cols], picked[:, cols], ident[:])
             col = sb.tile([P, PACK], F32, name="ts_col%d" % k)
-            nc.scalar.copy(out=col[:], in_=bank[k][:, 0:N:P])
+            nc.vector.tensor_copy(out=col[:], in_=bank[k][:, 0:N:P])
             for q in range(PACK):
                 cols = slice(q * P, (q + 1) * P)
-                nc.tensor.transpose(bank[2 + k][:, cols], col[:, q : q + 1].to_broadcast([P, P]), ident[:])
-            row = sb.tile([P, N], F32, name="ts_row%d" % k)
-            nc.scalar.copy(out=row[:], in_=bank[2 + k][:])
+                nc.tensor.transpose(bank[4 + k][:, cols], col[:, q : q + 1].to_broadcast([P, P]), ident[:])
             ts_col.append(col)
-            ts_row.append(row)
 
         xq_d = quantize("xq_d", x_by_d, E4M3)
-        window.append(sb.tile([P, T], F32, name="window3", tag="ts_window"))
-        nc.gpsimd.memset(window[3][:], 0.0)
+        clear_window(0, "ts_window")
 
         us_half = sb.tile([P, PACK], F32, name="us_half")
         c1_half = sb.tile([P, PACK], F32, name="c1_half")
@@ -141,10 +140,10 @@ def tile_attend_glwf_kernel(tc, xT, wT, us, ts, y, kp, w1, w2, offs, joffs, out)
             for j in range(PACK):
                 nc.tensor.transpose(bank[2 + u][:, j * P : (j + 1) * P], x_words[:, j, :, u], ident[:])
 
-        w_pairs = [sb.tile([P, 2 * T], BF16, name="w_pairs%d" % u) for u in range(2)]
+        w_pairs = [sb.tile([P, 2 * T], BF16, name="w_pairs%d" % u, tag="w_pairs%d" % u, align_bytes=64) for u in range(2)]
         w_new = sb.tile([P, PACK * N], BF16, name="w_new", align_bytes=64)
         w_old = sb.tile([P, PACK * N], BF16, name="w_old", align_bytes=64)
-        old_halves = sb.tile([P, 2, N], U32, name="old_halves")
+        old_words = w_old[:].bitcast(U32).rearrange("p (c u) -> p c u", u=2)
         new_words = w_new[:].bitcast(U32).rearrange("p (c u) -> p c u", u=2)
         for u, c0, raw in w_raw:
             dst = w_pairs[u][:, 2 * c0 : 2 * (c0 + W_CHUNK)].rearrange("p (c e) -> p c e", e=2)
@@ -158,13 +157,12 @@ def tile_attend_glwf_kernel(tc, xT, wT, us, ts, y, kp, w1, w2, offs, joffs, out)
                 nc.vector.tensor_copy(out=new_words[:, :, u], in_=words.indirect(new_list[:]))
                 if u == 1:
                     wq_new = quantize("wq_new", w_new, E4M3)
-                nc.vector.tensor_copy(out=old_halves[:, u, :], in_=words.indirect(old_list[:]))
-        nc.scalar.copy(
-            out=w_old[:].bitcast(U32).rearrange("p (c u) -> p c u", u=2),
-            in_=old_halves[:].rearrange("p u c -> p c u"),
-        )
-
-        x_by_r = sb.tile([P, PACK * D], BF16, name="x_by_r", align_bytes=64)
+                nc.vector.tensor_copy(out=old_words[:, :, u], in_=words.indirect(old_list[:]))
+        for k, slot in enumerate(("w_raw1_1024", "w_pairs1")):
+            row = sb.tile([P, N], F32, name="ts_row%d" % k, tag=slot, align_bytes=64)
+            nc.scalar.copy(out=row[:], in_=bank[4 + k][:])
+            ts_row.append(row)
+        x_by_r = sb.tile([P, PACK * D], BF16, name="x_by_r", tag="w_raw1_1536", align_bytes=64)
         for u in range(2):
             nc.scalar.copy(
                 out=x_by_r[:, u * 2 * D : (u + 1) * 2 * D].rearrange("s (e p j) -> s e p j", e=2, j=PACK),
@@ -182,9 +180,9 @@ def tile_attend_glwf_kernel(tc, xT, wT, us, ts, y, kp, w1, w2, offs, joffs, out)
                     is_transpose=True,
                 )
 
-        def finish_gradient(name, banks, col):
-            by_slot = sb.tile([P, PACK, R], BF16, name=name + "_by_slot")
-            grad = sb.tile([P, PACK * N], BF16, name=name + "_by_r", align_bytes=64)
+        def finish_gradient(name, banks, col, last_copy):
+            by_slot = sb.tile([P, PACK, R], BF16, name=name + "_by_slot", tag=name + "_by_slot", align_bytes=64)
+            grad = sb.tile([P, PACK * N], BF16, name=name + "_by_r", tag=name + "_by_r", align_bytes=64)
             grad_words = grad[:].bitcast(F32)
             for q in range(PACK):
                 nc.scalar.activation(
@@ -200,37 +198,37 @@ def tile_attend_glwf_kernel(tc, xT, wT, us, ts, y, kp, w1, w2, offs, joffs, out)
                         for u in range(2):
                             place = 2 * (qq % 2) + u
                             nc.tensor.transpose(back[:, place * P : (place + 1) * P], words[:, :, u], ident[:])
-            for half in range(2):
-                nc.scalar.copy(
+            for half, copy in enumerate((nc.scalar.copy, last_copy)):
+                copy(
                     out=grad_words[:, half * N : (half + 1) * N].rearrange("s (q p u) -> s q p u", q=2, u=2),
                     in_=banks[half][:].rearrange("s (q u p) -> s q p u", q=2, u=2),
                 )
             return quantize(name, grad, E5M2)
 
         g_banks = bank[4:8]
+        act = []
+        for j in range(PACK):
+            product(bank[j], xq_d, j, wq_new)
+            a_j = sb.tile([P, N], F32, name="a%d" % j, tag="a%d" % j)
+            nc.vector.tensor_tensor(a_j[:], bank[j][:], ts_row[0][:], ALU.mult)
+            nc.scalar.activation(out=a_j[:], in_=a_j[:], func=ACT.Tanh, scale=us_half[:, j : j + 1])
+            act.append(a_j)
         for j in range(PACK):
             nc.gpsimd.tensor_scalar(
                 y_sb[j][:], y_sb[j][:], c1_neg[:, j : j + 1], c1_half[:, j : j + 1], ALU.mult, ALU.add
             )
             add_turned(g_banks, y_sb[j], j, j == 0, False)
-        act = []
-        for j in range(PACK):
-            product(bank[j % 2], xq_d, j, wq_new)
-            a_j = sb.tile([P, N], F32, name="a%d" % j)
-            nc.vector.tensor_tensor(a_j[:], bank[j % 2][:], ts_row[0][:], ALU.mult)
-            nc.scalar.activation(out=a_j[:], in_=a_j[:], func=ACT.Tanh, scale=us_half[:, j : j + 1])
-            act.append(a_j)
         wq_old = quantize("wq_old", w_old, E4M3)
         for j in range(PACK):
             nc.vector.tensor_scalar(act[j][:], act[j][:], c1_half[:, j : j + 1], None, ALU.mult)
             add_turned(g_banks, act[j], j, False, j == PACK - 1)
         xq_r = quantize("xq_r", x_by_r, E4M3)
-        gq = finish_gradient("g", g_banks, ts_col[0])
+        gq = finish_gradient("g", g_banks, ts_col[0], nc.vector.tensor_copy)
 
         z = []
         neg_max = sb.tile([P, PACK], F32, name="neg_max")
         for j in range(PACK):
-            b_bank = bank[(j + 2) % 4]
+            b_bank = bank[j]
             product(b_bank, xq_d, j, wq_old)
             z_j = sb.tile([P, N], F32, name="z%d" % j)
             nc.vector.scalar_tensor_tensor(
@@ -240,36 +238,43 @@ def tile_attend_glwf_kernel(tc, xT, wT, us, ts, y, kp, w1, w2, offs, joffs, out)
         for j in range(PACK):
             nc.vector.tensor_reduce(neg_max[:, j : j + 1], z[j][:], AX.X, ALU.max, negate=True)
 
-        def place(name, grad_q, lst, t):
-            acc = bank[4 + (t + 2) % 4]
-            product(acc, xq_r, t, grad_q)
-            staged = sb.tile([P, N], F32, name="%s_staged%d" % (name, t))
-            nc.scalar.copy(out=staged[:], in_=acc[:])
+        def stage(name, acc, copy, slot):
+            staged = sb.tile([P, N], F32, name=name, tag=slot, align_bytes=64)
+            copy(out=staged[:], in_=acc[:])
+            return staged
+
+        def scatter(t, lst, staged):
             nc.vector.tensor_copy(out=window[t][:].indirect(lst[:]), in_=staged[:])
 
+        d1_banks = bank[0:3] + bank[7:8]
         for t in range(PACK):
-            place("d1", gq, new_list, t)
+            product(d1_banks[t], xq_r, t, gq)
+        for t in range(PACK - 1):
+            copy = nc.vector.tensor_copy if t == 0 else nc.scalar.copy
+            scatter(t, new_list, stage("d1_%d" % t, d1_banks[t], copy, "d1_%d" % t))
 
         h_banks = bank[0:4]
         total = sb.tile([P, PACK], F32, name="total")
-        e_scale = sb.tile([P, PACK], F32, name="e_scale")
+        inverse = sb.tile([P, PACK], F32, name="inverse")
+        e = sb.tile([P, PACK, N], F32, name="e", tag="g_by_slot", align_bytes=64)
         for j in range(PACK):
+            kept = sb.tile([P, N], F32, name="kept%d" % j, tag="a%d" % j)
+            nc.gpsimd.tensor_scalar(kept[:], kp_sb[:, j, :], c2_neg[:, j : j + 1], 0.0, ALU.mult, ALU.add)
+            add_turned(h_banks, kept, j, j == 0, False)
+        for j in range(PACK):
+            col = slice(j, j + 1)
             nc.scalar.activation(
-                out=z[j][:], in_=z[j][:], func=ACT.Exp, bias=neg_max[:, j : j + 1], accum_out=total[:, j : j + 1]
+                out=e[:, j, :], in_=z[j][:], func=ACT.Exp, bias=neg_max[:, col], accum_out=total[:, col]
             )
-        for j in range(PACK):
-            nc.gpsimd.tensor_scalar(
-                kp_sb[:, j, :], kp_sb[:, j, :], c2_neg[:, j : j + 1], 0.0, ALU.mult, ALU.add
-            )
-            add_turned(h_banks, kp_sb[:, j, :], j, j == 0, False)
-        nc.gpsimd.tensor_tensor(total[:], total[:], minus_one[:], ALU.pow)
-        nc.gpsimd.tensor_tensor(e_scale[:], total[:], c2[:], ALU.mult)
-        for j in range(PACK):
-            nc.scalar.activation(out=z[j][:], in_=z[j][:], func=ACT.Copy, scale=e_scale[:, j : j + 1])
+            nc.gpsimd.tensor_tensor(inverse[:, col], total[:, col], minus_one[:, col], ALU.pow)
+            nc.gpsimd.tensor_scalar(z[j][:], e[:, j, :], inverse[:, col], c2[:, col], ALU.mult, ALU.mult)
             add_turned(h_banks, z[j], j, False, j == PACK - 1)
-        hq = finish_gradient("h", h_banks, ts_col[1])
+        clear_window(3, "g_by_slot")
+        hq = finish_gradient("h", h_banks, ts_col[1], nc.scalar.copy)
+        scatter(3, new_list, stage("d1_3", d1_banks[3], nc.vector.tensor_copy, "h_by_r"))
 
         out_rows = out.rearrange("(p t) c -> p t c", t=PACK)
         for t in range(PACK):
-            place("d2", hq, old_list, t)
+            product(bank[4 + t], xq_r, t, hq)
+            scatter(t, old_list, stage("d2_%d" % t, bank[4 + t], nc.scalar.copy, "d2_%d" % t))
             nc.sync.dma_start(out=out_rows[:, t, :], in_=window[t][:])

@@ -9,6 +9,7 @@ FLOPS = 4 * 2 * D * R * N
 F32 = mybir.dt.float32
 BF16 = mybir.dt.bfloat16
 U32 = mybir.dt.uint32
+I32 = mybir.dt.int32
 U16 = mybir.dt.uint16
 U8 = mybir.dt.uint8
 E4M3 = mybir.dt.float8_e4m3fn_x4
@@ -47,93 +48,74 @@ def tile_attend_glwf_kernel(tc, xT, wT, us, ts, y, kp, w1, w2, offs, joffs, out)
                 stop=True,
             )
 
+        def zero(tile):
+            nc.vector.memset(tile[:].bitcast(I32), 0)
+
         ident = sb.tile([P, P], F32, name="ident")
         make_identity(nc, ident[:])
+        table_warm = sb.tile([P, 1], F32, name="table_warm")
+        nc.scalar.activation(out=table_warm[:], in_=ident[:, 0:1], func=ACT.Exp)
+
+        ts_window = sb.tile([P, T], F32, name="ts_window")
+        zero(ts_window)
+        nc.scalar.dma_start(out=ts_window[0:1, :], in_=ts[0:1, :])
 
         new_list = sb.tile([P, N // 16], U16, name="new_list")
         old_list = sb.tile([P, N // 16], U16, name="old_list")
-        x_raw = sb.tile([P, PACK, R], F32, name="x_raw", tag="x_raw", align_bytes=64)
-        nc.sync.dma_start(out=x_raw[:], in_=xT.rearrange("(p t) r -> p t r", t=PACK))
-        nc.sync.dma_start(new_list[:], offs)
-        nc.sync.dma_start(old_list[:], joffs)
-
-        ts_window = sb.tile([P, T], F32, name="ts_window", tag="ts_window", align_bytes=64)
-        nc.sync.dma_start(out=ts_window[0:32, :], in_=ts[0:32, :])
-        nc.gpsimd.memset(ts_window[32:64, :], 0.0)
-        nc.vector.memset(ts_window[64:128, :], 0.0)
-
+        x_raw = sb.tile([P, PACK, R], F32, name="x_raw")
         w_rows = wT.rearrange("(p t) c -> p t c", t=PACK)
-        w_raw = []
-        for u in range(2):
-            for c0 in range(0, T, W_CHUNK):
-                raw = sb.tile([P, 2, W_CHUNK], F32, name="w_raw%d_%d" % (u, c0), tag="w_raw%d_%d" % (u, c0), align_bytes=64)
-                nc.sync.dma_start(out=raw[:], in_=w_rows[:, 2 * u : 2 * u + 2, c0 : c0 + W_CHUNK])
-                w_raw.append((u, c0, raw))
+        w_raw = {}
 
+        def load_w(u, c0):
+            slot = "w_raw%d_%d" % (u, c0)
+            w_raw[u, c0] = sb.tile([P, 2, W_CHUNK], F32, name=slot, tag=slot, align_bytes=64)
+            nc.sync.dma_start(out=w_raw[u, c0][:], in_=w_rows[:, 2 * u : 2 * u + 2, c0 : c0 + W_CHUNK])
+
+        nc.sync.dma_start(out=x_raw[:], in_=xT.rearrange("(p t) r -> p t r", t=PACK))
+        nc.sync.dma_start(old_list[:], joffs)
+        nc.sync.dma_start(new_list[:], offs)
+        for c0 in range(0, T, W_CHUNK):
+            load_w(0, c0)
         row_vec = {}
         for name, src in (("us", us), ("w1", w1), ("w2", w2)):
             row_vec[name] = sb.tile([P, PACK], F32, name=name + "_rows")
             nc.sync.dma_start(out=row_vec[name][:], in_=src.rearrange("(p j) o -> p (j o)", j=PACK))
+        for c0 in range(0, T, W_CHUNK):
+            load_w(1, c0)
+        kp_rows = kp.rearrange("(p j) i -> p j i", j=PACK)
+        kp_sb = []
+        for half in range(2):
+            kp_half = sb.tile([P, 2, N], F32, name="kp%d" % half)
+            nc.sync.dma_start(out=kp_half[:], in_=kp_rows[:, 2 * half : 2 * half + 2, :])
+            kp_sb.extend([kp_half[:, 0, :], kp_half[:, 1, :]])
+        y_sb = sb.tile([P, PACK, N], F32, name="y_sb")
+        nc.sync.dma_start(out=y_sb[:], in_=y.rearrange("(p j) i -> p j i", j=PACK))
 
-        y_rows = y.rearrange("(p j) i -> p j i", j=PACK)
-        y_sb = []
-        for j in range(PACK):
-            y_j = sb.tile([P, N], F32, name="y%d" % j)
-            nc.sync.dma_start(out=y_j[:], in_=y_rows[:, j, :])
-            y_sb.append(y_j)
-        kp_sb = sb.tile([P, PACK, N], F32, name="kp_sb")
-        nc.sync.dma_start(out=kp_sb[:], in_=kp.rearrange("(p j) i -> p j i", j=PACK))
-
-        table_warm = sb.tile([P, 1], F32, name="table_warm")
-        nc.scalar.activation(out=table_warm[:], in_=ident[:, 0:1], func=ACT.Exp)
-
-        window = {}
-
-        def clear_window(t, slot):
-            window[t] = sb.tile([P, T], F32, name="window%d" % t, tag=slot, align_bytes=64)
-            nc.gpsimd.memset(window[t][:], 0.0)
-
-        window[2] = sb.tile([P, T], F32, name="window2")
-        nc.vector.memset(window[2][:], 0.0)
+        window = []
+        for t in range(PACK):
+            window.append(sb.tile([P, T], F32, name="window%d" % t))
+            zero(window[t])
 
         x_by_d = sb.tile([P, PACK * R], BF16, name="x_by_d", align_bytes=64)
-        nc.vector.tensor_copy(
-            out=x_by_d[:].rearrange("p (j s t) -> p j s t", j=PACK, t=PACK),
-            in_=x_raw[:].rearrange("p t (s j) -> p j s t", j=PACK),
-        )
+        dealt = x_by_d[:].rearrange("p (j s t) -> p j s t", j=PACK, t=PACK)
+        x_cols = x_raw[:].rearrange("p t (s j) -> p j s t", j=PACK)
+        nc.vector.tensor_copy(out=dealt[:, 0:3], in_=x_cols[:, 0:3])
+        nc.scalar.copy(out=dealt[:, 3], in_=x_cols[:, 3])
 
-        clear_window(1, "x_raw")
-
-        ts_col = []
-        ts_row = []
-        for k, lst in enumerate((new_list, old_list)):
-            picked = sb.tile([P, N], F32, name="ts_picked%d" % k)
+        ts_col = {}
+        for k, (name, lst) in enumerate((("old", old_list), ("new", new_list))):
+            picked = sb.tile([P, N], F32, name="ts_picked_" + name)
             nc.vector.tensor_copy(out=picked[:], in_=ts_window[:].indirect(lst[:]))
             for q in range(PACK):
                 cols = slice(q * P, (q + 1) * P)
                 nc.tensor.transpose(bank[k][:, cols], picked[:, cols], ident[:])
-            col = sb.tile([P, PACK], F32, name="ts_col%d" % k)
-            nc.vector.tensor_copy(out=col[:], in_=bank[k][:, 0:N:P])
+            ts_col[name] = sb.tile([P, PACK], F32, name="ts_col_" + name)
+        xq_d = quantize("xq_d", x_by_d, E4M3)
+        for k, name in enumerate(("old", "new")):
+            nc.vector.tensor_copy(out=ts_col[name][:], in_=bank[k][:, 0:N:P])
             for q in range(PACK):
                 cols = slice(q * P, (q + 1) * P)
-                nc.tensor.transpose(bank[4 + k][:, cols], col[:, q : q + 1].to_broadcast([P, P]), ident[:])
-            ts_col.append(col)
-
-        xq_d = quantize("xq_d", x_by_d, E4M3)
-        clear_window(0, "ts_window")
-
-        us_half = sb.tile([P, PACK], F32, name="us_half")
-        c1_half = sb.tile([P, PACK], F32, name="c1_half")
-        c1_neg = sb.tile([P, PACK], F32, name="c1_neg")
-        c2 = sb.tile([P, PACK], F32, name="c2")
-        c2_neg = sb.tile([P, PACK], F32, name="c2_neg")
-        minus_one = sb.tile([P, PACK], F32, name="minus_one")
-        nc.gpsimd.memset(minus_one[:], -1.0)
-        nc.gpsimd.tensor_scalar(us_half[:], row_vec["us"][:], 0.5, 0.0, ALU.mult, ALU.add)
-        nc.gpsimd.tensor_tensor(c1_half[:], row_vec["w1"][:], us_half[:], ALU.mult)
-        nc.gpsimd.tensor_scalar(c1_neg[:], c1_half[:], -2.0, 0.0, ALU.mult, ALU.add)
-        nc.gpsimd.tensor_tensor(c2[:], row_vec["w2"][:], row_vec["us"][:], ALU.mult)
-        nc.gpsimd.tensor_scalar(c2_neg[:], c2[:], -1.0, 0.0, ALU.mult, ALU.add)
+                nc.tensor.transpose(bank[4 + k][:, cols], ts_col[name][:, q : q + 1].to_broadcast([P, P]), ident[:])
 
         x_words = x_by_d[:].bitcast(F32).rearrange("p (j s u) -> p j s u", j=PACK, u=2)
         for u in range(2):
@@ -142,32 +124,64 @@ def tile_attend_glwf_kernel(tc, xT, wT, us, ts, y, kp, w1, w2, offs, joffs, out)
 
         w_pairs = [sb.tile([P, 2 * T], BF16, name="w_pairs%d" % u, tag="w_pairs%d" % u, align_bytes=64) for u in range(2)]
         w_new = sb.tile([P, PACK * N], BF16, name="w_new", align_bytes=64)
-        w_old = sb.tile([P, PACK * N], BF16, name="w_old", align_bytes=64)
-        old_words = w_old[:].bitcast(U32).rearrange("p (c u) -> p c u", u=2)
-        new_words = w_new[:].bitcast(U32).rearrange("p (c u) -> p c u", u=2)
-        for u, c0, raw in w_raw:
+        w_old = sb.tile([P, PACK * N], BF16, name="w_old", tag="w_old", align_bytes=64)
+
+        def cast_w(u, c0):
             dst = w_pairs[u][:, 2 * c0 : 2 * (c0 + W_CHUNK)].rearrange("p (c e) -> p c e", e=2)
-            src = raw[:].rearrange("p e c -> p c e")
+            src = w_raw[u, c0][:].rearrange("p e c -> p c e")
             if u == 1 and c0 + W_CHUNK == T:
                 nc.vector.tensor_copy(out=dst, in_=src)
             else:
                 nc.scalar.activation(out=dst, in_=src, func=ACT.Copy)
-            if c0 + W_CHUNK == T:
-                words = w_pairs[u][:].bitcast(U32)
-                nc.vector.tensor_copy(out=new_words[:, :, u], in_=words.indirect(new_list[:]))
-                if u == 1:
-                    wq_new = quantize("wq_new", w_new, E4M3)
-                nc.vector.tensor_copy(out=old_words[:, :, u], in_=words.indirect(old_list[:]))
-        for k, slot in enumerate(("w_raw1_1024", "w_pairs1")):
-            row = sb.tile([P, N], F32, name="ts_row%d" % k, tag=slot, align_bytes=64)
-            nc.scalar.copy(out=row[:], in_=bank[4 + k][:])
-            ts_row.append(row)
+
+        old_pairs = sb.tile([P, 2, N], U32, name="old_pairs")
+        new_pairs = sb.tile([P, 2, N], U32, name="new_pairs")
+
+        def gather_w(dst, u, lst):
+            nc.vector.tensor_copy(out=dst[:, u, :], in_=w_pairs[u][:].bitcast(U32).indirect(lst[:]))
+
+        def weave(copy, word, dst, pairs):
+            copy(
+                out=dst[:].bitcast(word).rearrange("p (c u) -> p c u", u=2),
+                in_=pairs[:].bitcast(word).rearrange("p u c -> p c u"),
+            )
+
+        for c0 in range(0, T, W_CHUNK):
+            cast_w(0, c0)
+        gather_w(old_pairs, 0, old_list)
+        gather_w(new_pairs, 0, new_list)
+
+        us_half = sb.tile([P, PACK], F32, name="us_half")
+        c1_half = sb.tile([P, PACK], F32, name="c1_half")
+        c1_neg = sb.tile([P, PACK], F32, name="c1_neg")
+        c2 = sb.tile([P, PACK], F32, name="c2")
+        nc.vector.tensor_tensor(c2[:], row_vec["w2"][:], row_vec["us"][:], ALU.mult)
+        nc.vector.tensor_scalar(us_half[:], row_vec["us"][:], 0.5, None, ALU.mult)
+        nc.vector.scalar_tensor_tensor(c1_half[:], row_vec["w1"][:], 0.5, row_vec["us"][:], ALU.mult, ALU.mult)
+        nc.vector.scalar_tensor_tensor(c1_neg[:], row_vec["w1"][:], -1.0, row_vec["us"][:], ALU.mult, ALU.mult)
+
+        for c0 in range(0, T, W_CHUNK):
+            cast_w(1, c0)
+        gather_w(old_pairs, 1, old_list)
+        weave(nc.vector.tensor_copy, I32, w_old, old_pairs)
+        wq_old = quantize("wq_old", w_old, E4M3)
+        gather_w(new_pairs, 1, new_list)
+
+        ts_row = {}
+
+        def spread_ts(name, src, slot):
+            ts_row[name] = sb.tile([P, N], F32, name="ts_row_" + name, tag=slot, align_bytes=64)
+            nc.scalar.copy(out=ts_row[name][:], in_=src[:])
+
+        spread_ts("old", bank[4], "w_raw1_1024")
         x_by_r = sb.tile([P, PACK * D], BF16, name="x_by_r", tag="w_raw1_1536", align_bytes=64)
         for u in range(2):
             nc.scalar.copy(
                 out=x_by_r[:, u * 2 * D : (u + 1) * 2 * D].rearrange("s (e p j) -> s e p j", e=2, j=PACK),
                 in_=bank[2 + u][:].bitcast(BF16).rearrange("s (j p e) -> s e p j", j=PACK, e=2),
             )
+        spread_ts("new", bank[5], "w_pairs1")
+        weave(nc.scalar.copy, U32, w_new, new_pairs)
 
         def add_turned(banks, src, j, first, last):
             for q in range(PACK):
@@ -180,17 +194,17 @@ def tile_attend_glwf_kernel(tc, xT, wT, us, ts, y, kp, w1, w2, offs, joffs, out)
                     is_transpose=True,
                 )
 
-        def finish_gradient(name, banks, col, last_copy):
-            by_slot = sb.tile([P, PACK, R], BF16, name=name + "_by_slot", tag=name + "_by_slot", align_bytes=64)
+        def finish_gradient(name, banks, col, vector_helps):
+            by_slot = sb.tile([P, PACK, R], BF16, name=name + "_by_slot")
             grad = sb.tile([P, PACK * N], BF16, name=name + "_by_r", tag=name + "_by_r", align_bytes=64)
             grad_words = grad[:].bitcast(F32)
             for q in range(PACK):
-                nc.scalar.activation(
-                    out=by_slot[:, q, :].rearrange("p (s j) -> p s j", j=PACK),
-                    in_=banks[q][:].rearrange("p (j s) -> p s j", j=PACK),
-                    func=ACT.Copy,
-                    scale=col[:, q : q + 1],
-                )
+                dst = by_slot[:, q, :].rearrange("p (s j) -> p s j", j=PACK)
+                src = banks[q][:].rearrange("p (j s) -> p s j", j=PACK)
+                if vector_helps and q % 2 == 1:
+                    nc.vector.tensor_scalar(dst, src, col[:, q : q + 1], None, ALU.mult)
+                else:
+                    nc.scalar.activation(out=dst, in_=src, func=ACT.Copy, scale=col[:, q : q + 1])
                 if q % 2 == 1:
                     back = banks[q // 2]
                     for qq in (q - 1, q):
@@ -198,45 +212,62 @@ def tile_attend_glwf_kernel(tc, xT, wT, us, ts, y, kp, w1, w2, offs, joffs, out)
                         for u in range(2):
                             place = 2 * (qq % 2) + u
                             nc.tensor.transpose(back[:, place * P : (place + 1) * P], words[:, :, u], ident[:])
-            for half, copy in enumerate((nc.scalar.copy, last_copy)):
+            for half in range(2):
+                copy = nc.vector.tensor_copy if vector_helps and half == 1 else nc.scalar.copy
                 copy(
                     out=grad_words[:, half * N : (half + 1) * N].rearrange("s (q p u) -> s q p u", q=2, u=2),
                     in_=banks[half][:].rearrange("s (q u p) -> s q p u", q=2, u=2),
                 )
             return quantize(name, grad, E5M2)
 
-        g_banks = bank[4:8]
+        h_banks = bank[4:8]
+        neg_max = sb.tile([P, PACK], F32, name="neg_max")
+        total = sb.tile([P, PACK], F32, name="total")
+        inverse = sb.tile([P, PACK], F32, name="inverse")
+        e_scale = sb.tile([P, PACK], F32, name="e_scale")
+        z = [sb.tile([P, N], F32, name="z%d" % j, tag="z%d" % j) for j in range(PACK)]
+
+        def score(j):
+            nc.vector.scalar_tensor_tensor(
+                z[j][:], bank[j][:], row_vec["us"][:, j : j + 1], ts_row["old"][:], ALU.mult, ALU.mult
+            )
+
+        def exponentiate(j):
+            col = slice(j, j + 1)
+            nc.vector.tensor_reduce(neg_max[:, col], z[j][:], AX.X, ALU.max, negate=True)
+            nc.scalar.activation(
+                out=z[j][:], in_=z[j][:], func=ACT.Exp, bias=neg_max[:, col], accum_out=total[:, col]
+            )
+
+        def normalise(j):
+            col = slice(j, j + 1)
+            nc.vector.reciprocal(inverse[:, col], total[:, col])
+            nc.vector.tensor_tensor(e_scale[:, col], inverse[:, col], c2[:, col], ALU.mult)
+            nc.scalar.activation(out=z[j][:], in_=z[j][:], func=ACT.Copy, scale=e_scale[:, col])
+            add_turned(h_banks, z[j], j, False, j == PACK - 1)
+
+        for j in range(PACK):
+            product(bank[j], xq_d, j, wq_old)
+        kept = sb.tile([P, PACK, N], F32, name="kept", tag="w_old", align_bytes=64)
+        for j in range(PACK):
+            nc.gpsimd.tensor_scalar(kept[:, j, :], kp_sb[j], c2[:, j : j + 1], -1.0, ALU.mult, ALU.mult)
+            add_turned(h_banks, kept[:, j, :], j, j == 0, False)
+        for step in range(PACK + 2):
+            if step < PACK:
+                score(step)
+            if 1 <= step <= PACK:
+                exponentiate(step - 1)
+            if step >= 2:
+                normalise(step - 2)
+        xq_r = quantize("xq_r", x_by_r, E4M3)
+        hq = finish_gradient("h", h_banks, ts_col["old"], True)
+
+        wq_new = quantize("wq_new", w_new, E4M3)
         act = []
         for j in range(PACK):
             product(bank[j], xq_d, j, wq_new)
-            a_j = sb.tile([P, N], F32, name="a%d" % j, tag="a%d" % j)
-            nc.vector.tensor_tensor(a_j[:], bank[j][:], ts_row[0][:], ALU.mult)
-            nc.scalar.activation(out=a_j[:], in_=a_j[:], func=ACT.Tanh, scale=us_half[:, j : j + 1])
-            act.append(a_j)
-        for j in range(PACK):
-            nc.gpsimd.tensor_scalar(
-                y_sb[j][:], y_sb[j][:], c1_neg[:, j : j + 1], c1_half[:, j : j + 1], ALU.mult, ALU.add
-            )
-            add_turned(g_banks, y_sb[j], j, j == 0, False)
-        wq_old = quantize("wq_old", w_old, E4M3)
-        for j in range(PACK):
-            nc.vector.tensor_scalar(act[j][:], act[j][:], c1_half[:, j : j + 1], None, ALU.mult)
-            add_turned(g_banks, act[j], j, False, j == PACK - 1)
-        xq_r = quantize("xq_r", x_by_r, E4M3)
-        gq = finish_gradient("g", g_banks, ts_col[0], nc.vector.tensor_copy)
-
-        z = []
-        neg_max = sb.tile([P, PACK], F32, name="neg_max")
-        for j in range(PACK):
-            b_bank = bank[j]
-            product(b_bank, xq_d, j, wq_old)
-            z_j = sb.tile([P, N], F32, name="z%d" % j)
-            nc.vector.scalar_tensor_tensor(
-                z_j[:], b_bank[:], row_vec["us"][:, j : j + 1], ts_row[1][:], ALU.mult, ALU.mult
-            )
-            z.append(z_j)
-        for j in range(PACK):
-            nc.vector.tensor_reduce(neg_max[:, j : j + 1], z[j][:], AX.X, ALU.max, negate=True)
+            act.append(sb.tile([P, N], F32, name="a%d" % j))
+            nc.vector.tensor_tensor(act[j][:], bank[j][:], ts_row["new"][:], ALU.mult)
 
         def stage(name, acc, copy, slot):
             staged = sb.tile([P, N], F32, name=name, tag=slot, align_bytes=64)
@@ -246,35 +277,28 @@ def tile_attend_glwf_kernel(tc, xT, wT, us, ts, y, kp, w1, w2, offs, joffs, out)
         def scatter(t, lst, staged):
             nc.vector.tensor_copy(out=window[t][:].indirect(lst[:]), in_=staged[:])
 
-        d1_banks = bank[0:3] + bank[7:8]
+        d2_banks = bank[6:8] + bank[4:6]
         for t in range(PACK):
-            product(d1_banks[t], xq_r, t, gq)
+            product(d2_banks[t], xq_r, t, hq)
         for t in range(PACK - 1):
-            copy = nc.vector.tensor_copy if t == 0 else nc.scalar.copy
-            scatter(t, new_list, stage("d1_%d" % t, d1_banks[t], copy, "d1_%d" % t))
+            scatter(t, old_list, stage("d2_%d" % t, d2_banks[t], nc.scalar.copy, "d2_%d" % t))
 
-        h_banks = bank[0:4]
-        total = sb.tile([P, PACK], F32, name="total")
-        inverse = sb.tile([P, PACK], F32, name="inverse")
-        e = sb.tile([P, PACK, N], F32, name="e", tag="g_by_slot", align_bytes=64)
+        g_banks = bank[0:4]
+        target = sb.tile([P, PACK, N], F32, name="target", tag="z3")
         for j in range(PACK):
-            kept = sb.tile([P, N], F32, name="kept%d" % j, tag="a%d" % j)
-            nc.gpsimd.tensor_scalar(kept[:], kp_sb[:, j, :], c2_neg[:, j : j + 1], 0.0, ALU.mult, ALU.add)
-            add_turned(h_banks, kept, j, j == 0, False)
+            nc.gpsimd.tensor_scalar(target[:, j, :], y_sb[:, j, :], -0.5, c1_neg[:, j : j + 1], ALU.add, ALU.mult)
+            add_turned(g_banks, target[:, j, :], j, j == 0, False)
         for j in range(PACK):
             col = slice(j, j + 1)
-            nc.scalar.activation(
-                out=e[:, j, :], in_=z[j][:], func=ACT.Exp, bias=neg_max[:, col], accum_out=total[:, col]
-            )
-            nc.gpsimd.tensor_tensor(inverse[:, col], total[:, col], minus_one[:, col], ALU.pow)
-            nc.gpsimd.tensor_scalar(z[j][:], e[:, j, :], inverse[:, col], c2[:, col], ALU.mult, ALU.mult)
-            add_turned(h_banks, z[j], j, False, j == PACK - 1)
-        clear_window(3, "g_by_slot")
-        hq = finish_gradient("h", h_banks, ts_col[1], nc.scalar.copy)
-        scatter(3, new_list, stage("d1_3", d1_banks[3], nc.vector.tensor_copy, "h_by_r"))
+            nc.scalar.activation(out=act[j][:], in_=act[j][:], func=ACT.Tanh, scale=us_half[:, col])
+            nc.scalar.activation(out=act[j][:], in_=act[j][:], func=ACT.Copy, scale=c1_half[:, col])
+            add_turned(g_banks, act[j], j, False, j == PACK - 1)
+        gq = finish_gradient("g", g_banks, ts_col["new"], False)
+        scatter(3, old_list, stage("d2_3", d2_banks[3], nc.vector.tensor_copy, "g_by_r"))
 
         out_rows = out.rearrange("(p t) c -> p t c", t=PACK)
+        d1_banks = bank[6:8] + bank[4:5] + bank[2:3]
         for t in range(PACK):
-            product(bank[4 + t], xq_r, t, hq)
-            scatter(t, old_list, stage("d2_%d" % t, bank[4 + t], nc.scalar.copy, "d2_%d" % t))
+            product(d1_banks[t], xq_r, t, gq)
+            scatter(t, new_list, stage("d1_%d" % t, d1_banks[t], nc.scalar.copy, "d1_%d" % t))
             nc.sync.dma_start(out=out_rows[:, t, :], in_=window[t][:])

@@ -30,8 +30,8 @@ def tile_attend_glwf_kernel(tc, xT, wT, us, ts, y, kp, w1, w2, offs, joffs, out)
         ps = ctx.enter_context(tc.psum_pool(name="ps", bufs=1))
         bank = [ps.tile([P, N], F32, name="bank%d" % b) for b in range(8)]
 
-        def quantize(name, src, fmt):
-            codes = sb.tile([P, N], U32, name=name + "_codes", tag=name + "_codes", align_bytes=64)
+        def quantize(name, src, fmt, slot=None):
+            codes = sb.tile([P, N], U32, name=name + "_codes", tag=slot or name, align_bytes=64)
             scales = sb.tile([P, N], U8, name=name + "_scales", align_bytes=64)
             nc.vector.quantize_mx(out=codes[:].bitcast(fmt), scales=scales[:], in_=src[:])
             return codes, scales, fmt
@@ -92,7 +92,7 @@ def tile_attend_glwf_kernel(tc, xT, wT, us, ts, y, kp, w1, w2, offs, joffs, out)
         nc.sync.dma_start(out=y_sb[:], in_=y.rearrange("(p j) i -> p j i", j=PACK))
 
         window = []
-        for t in range(PACK):
+        for t in range(PACK - 1):
             window.append(sb.tile([P, T], F32, name="window%d" % t))
             zero(window[t])
 
@@ -134,22 +134,16 @@ def tile_attend_glwf_kernel(tc, xT, wT, us, ts, y, kp, w1, w2, offs, joffs, out)
             else:
                 nc.scalar.activation(out=dst, in_=src, func=ACT.Copy)
 
-        old_pairs = sb.tile([P, 2, N], U32, name="old_pairs")
-        new_pairs = sb.tile([P, 2, N], U32, name="new_pairs")
+        old_pairs = sb.tile([P, 2, N], U32, name="old_pairs", tag="old_pairs", align_bytes=64)
+        new_words = w_new[:].bitcast(U32).rearrange("p (c u) -> p c u", u=2)
 
         def gather_w(dst, u, lst):
-            nc.vector.tensor_copy(out=dst[:, u, :], in_=w_pairs[u][:].bitcast(U32).indirect(lst[:]))
-
-        def weave(copy, word, dst, pairs):
-            copy(
-                out=dst[:].bitcast(word).rearrange("p (c u) -> p c u", u=2),
-                in_=pairs[:].bitcast(word).rearrange("p u c -> p c u"),
-            )
+            nc.vector.tensor_copy(out=dst, in_=w_pairs[u][:].bitcast(U32).indirect(lst[:]))
 
         for c0 in range(0, T, W_CHUNK):
             cast_w(0, c0)
-        gather_w(old_pairs, 0, old_list)
-        gather_w(new_pairs, 0, new_list)
+        gather_w(old_pairs[:, 0, :], 0, old_list)
+        gather_w(new_words[:, :, 0], 0, new_list)
 
         us_half = sb.tile([P, PACK], F32, name="us_half")
         c1_half = sb.tile([P, PACK], F32, name="c1_half")
@@ -162,10 +156,14 @@ def tile_attend_glwf_kernel(tc, xT, wT, us, ts, y, kp, w1, w2, offs, joffs, out)
 
         for c0 in range(0, T, W_CHUNK):
             cast_w(1, c0)
-        gather_w(old_pairs, 1, old_list)
-        weave(nc.vector.tensor_copy, I32, w_old, old_pairs)
+        gather_w(old_pairs[:, 1, :], 1, old_list)
+        nc.vector.tensor_copy(
+            out=w_old[:].bitcast(I32).rearrange("p (c u) -> p c u", u=2),
+            in_=old_pairs[:].bitcast(I32).rearrange("p u c -> p c u"),
+        )
         wq_old = quantize("wq_old", w_old, E4M3)
-        gather_w(new_pairs, 1, new_list)
+        new_upper = sb.tile([P, N], U32, name="new_upper", tag="w_old", align_bytes=64)
+        gather_w(new_upper[:], 1, new_list)
 
         ts_row = {}
 
@@ -180,8 +178,8 @@ def tile_attend_glwf_kernel(tc, xT, wT, us, ts, y, kp, w1, w2, offs, joffs, out)
                 out=x_by_r[:, u * 2 * D : (u + 1) * 2 * D].rearrange("s (e p j) -> s e p j", e=2, j=PACK),
                 in_=bank[2 + u][:].bitcast(BF16).rearrange("s (j p e) -> s e p j", j=PACK, e=2),
             )
-        spread_ts("new", bank[5], "w_pairs1")
-        weave(nc.scalar.copy, U32, w_new, new_pairs)
+        spread_ts("new", bank[5], "old_pairs")
+        nc.scalar.copy(out=new_words[:, :, 1], in_=new_upper[:])
 
         def add_turned(banks, src, j, first, last):
             for q in range(PACK):
@@ -201,7 +199,7 @@ def tile_attend_glwf_kernel(tc, xT, wT, us, ts, y, kp, w1, w2, offs, joffs, out)
             for q in range(PACK):
                 dst = by_slot[:, q, :].rearrange("p (s j) -> p s j", j=PACK)
                 src = banks[q][:].rearrange("p (j s) -> p s j", j=PACK)
-                if vector_helps and q % 2 == 1:
+                if vector_helps and q == PACK - 1:
                     nc.vector.tensor_scalar(dst, src, col[:, q : q + 1], None, ALU.mult)
                 else:
                     nc.scalar.activation(out=dst, in_=src, func=ACT.Copy, scale=col[:, q : q + 1])
@@ -213,18 +211,16 @@ def tile_attend_glwf_kernel(tc, xT, wT, us, ts, y, kp, w1, w2, offs, joffs, out)
                             place = 2 * (qq % 2) + u
                             nc.tensor.transpose(back[:, place * P : (place + 1) * P], words[:, :, u], ident[:])
             for half in range(2):
-                copy = nc.vector.tensor_copy if vector_helps and half == 1 else nc.scalar.copy
-                copy(
+                nc.scalar.copy(
                     out=grad_words[:, half * N : (half + 1) * N].rearrange("s (q p u) -> s q p u", q=2, u=2),
                     in_=banks[half][:].rearrange("s (q u p) -> s q p u", q=2, u=2),
                 )
             return quantize(name, grad, E5M2)
 
         h_banks = bank[4:8]
-        neg_max = sb.tile([P, PACK], F32, name="neg_max")
-        total = sb.tile([P, PACK], F32, name="total")
-        inverse = sb.tile([P, PACK], F32, name="inverse")
-        e_scale = sb.tile([P, PACK], F32, name="e_scale")
+        neg_max = sb.tile([P, PACK], F32, name="neg_max", tag="neg_max", align_bytes=64)
+        total = sb.tile([P, PACK], F32, name="total", tag="total")
+        inverse = sb.tile([P, PACK], F32, name="inverse", tag="inverse", align_bytes=64)
         z = [sb.tile([P, N], F32, name="z%d" % j, tag="z%d" % j) for j in range(PACK)]
 
         def score(j):
@@ -239,30 +235,33 @@ def tile_attend_glwf_kernel(tc, xT, wT, us, ts, y, kp, w1, w2, offs, joffs, out)
                 out=z[j][:], in_=z[j][:], func=ACT.Exp, bias=neg_max[:, col], accum_out=total[:, col]
             )
 
-        def normalise(j):
-            col = slice(j, j + 1)
-            nc.vector.reciprocal(inverse[:, col], total[:, col])
-            nc.vector.tensor_tensor(e_scale[:, col], inverse[:, col], c2[:, col], ALU.mult)
-            nc.scalar.activation(out=z[j][:], in_=z[j][:], func=ACT.Copy, scale=e_scale[:, col])
-            add_turned(h_banks, z[j], j, False, j == PACK - 1)
+        def normalise(tiles):
+            cols = slice(tiles[0], tiles[-1] + 1)
+            nc.vector.reciprocal(inverse[:, cols], total[:, cols])
+            for j in tiles:
+                col = slice(j, j + 1)
+                nc.vector.tensor_scalar(z[j][:], z[j][:], inverse[:, col], c2[:, col], ALU.mult, ALU.mult)
+                add_turned(h_banks, z[j], j, False, j == PACK - 1)
 
         for j in range(PACK):
             product(bank[j], xq_d, j, wq_old)
-        kept = sb.tile([P, PACK, N], F32, name="kept", tag="w_old", align_bytes=64)
+        kept = sb.tile([P, PACK, N], F32, name="kept", tag="w_pairs1", align_bytes=64)
         for j in range(PACK):
             nc.gpsimd.tensor_scalar(kept[:, j, :], kp_sb[j], c2[:, j : j + 1], -1.0, ALU.mult, ALU.mult)
             add_turned(h_banks, kept[:, j, :], j, j == 0, False)
-        for step in range(PACK + 2):
+        for step in range(PACK + 1):
             if step < PACK:
                 score(step)
-            if 1 <= step <= PACK:
+            if step >= 1:
                 exponentiate(step - 1)
-            if step >= 2:
-                normalise(step - 2)
-        xq_r = quantize("xq_r", x_by_r, E4M3)
+        normalise([0, 1, 2])
+        normalise([3])
+        xq_r = quantize("xq_r", x_by_r, E4M3, "inverse")
         hq = finish_gradient("h", h_banks, ts_col["old"], True)
 
-        wq_new = quantize("wq_new", w_new, E4M3)
+        wq_new = quantize("wq_new", w_new, E4M3, "neg_max")
+        window.append(sb.tile([P, T], F32, name="window3", tag="total"))
+        zero(window[3])
         act = []
         for j in range(PACK):
             product(bank[j], xq_d, j, wq_new)

from contextlib import ExitStack

import concourse.mybir as mybir
from concourse.masks import make_identity

D, R, N, T = 512, 512, 512, 2048
FLOPS = 4 * 2 * D * R * N

F32 = mybir.dt.float32
BF16 = mybir.dt.bfloat16
U32 = mybir.dt.uint32
I32 = mybir.dt.int32
U16 = mybir.dt.uint16
U8 = mybir.dt.uint8
E4M3 = mybir.dt.float8_e4m3fn_x4
E5M2 = mybir.dt.float8_e5m2_x4
ALU = mybir.AluOpType
ACT = mybir.ActivationFunctionType
AX = mybir.AxisListType

P = 128
PACK = 4
W_CHUNK = 512


def tile_attend_glwf_kernel(tc, xT, wT, us, ts, y, kp, w1, w2, offs, joffs, out):
    nc = tc.nc
    with ExitStack() as ctx:
        sb = ctx.enter_context(tc.tile_pool(name="sb", bufs=1))
        ps = ctx.enter_context(tc.psum_pool(name="ps", bufs=1))
        bank = [ps.tile([P, N], F32, name="bank%d" % b) for b in range(8)]

        def quantize(name, src, fmt, slot=None):
            codes = sb.tile([P, N], U32, name=name + "_codes", tag=slot or name, align_bytes=64)
            scales = sb.tile([P, N], U8, name=name + "_scales", align_bytes=64)
            nc.vector.quantize_mx(out=codes[:].bitcast(fmt), scales=scales[:], in_=src[:])
            return codes, scales, fmt

        def product(dst, stat, block, mov):
            cols = slice(block * P, (block + 1) * P)
            nc.tensor.matmul_mx(
                out=dst[:],
                lhsT=stat[0][:, cols].bitcast(stat[2]),
                lhsT_scale=stat[1][:, cols],
                rhs=mov[0][:].bitcast(mov[2]),
                rhs_scale=mov[1][:],
                start=True,
                stop=True,
            )

        def zero(tile):
            nc.vector.memset(tile[:].bitcast(I32), 0)

        ident = sb.tile([P, P], F32, name="ident")
        make_identity(nc, ident[:])
        table_warm = sb.tile([P, 1], F32, name="table_warm")
        nc.scalar.activation(out=table_warm[:], in_=ident[:, 0:1], func=ACT.Exp)

        ts_window = sb.tile([P, T], F32, name="ts_window")
        zero(ts_window)
        nc.scalar.dma_start(out=ts_window[0:1, :], in_=ts[0:1, :])

        new_list = sb.tile([P, N // 16], U16, name="new_list")
        old_list = sb.tile([P, N // 16], U16, name="old_list")
        x_raw = sb.tile([P, PACK, R], F32, name="x_raw")
        w_rows = wT.rearrange("(p t) c -> p t c", t=PACK)
        w_raw = {}

        def load_w(u, c0):
            slot = "w_raw%d_%d" % (u, c0)
            w_raw[u, c0] = sb.tile([P, 2, W_CHUNK], F32, name=slot, tag=slot, align_bytes=64)
            nc.sync.dma_start(out=w_raw[u, c0][:], in_=w_rows[:, 2 * u : 2 * u + 2, c0 : c0 + W_CHUNK])

        nc.sync.dma_start(out=x_raw[:], in_=xT.rearrange("(p t) r -> p t r", t=PACK))
        nc.sync.dma_start(old_list[:], joffs)
        nc.sync.dma_start(new_list[:], offs)
        for c0 in range(0, T, W_CHUNK):
            load_w(0, c0)
        row_vec = {}
        for name, src in (("us", us), ("w1", w1), ("w2", w2)):
            row_vec[name] = sb.tile([P, PACK], F32, name=name + "_rows")
            nc.sync.dma_start(out=row_vec[name][:], in_=src.rearrange("(p j) o -> p (j o)", j=PACK))
        for c0 in range(0, T, W_CHUNK):
            load_w(1, c0)
        kp_rows = kp.rearrange("(p j) i -> p j i", j=PACK)
        kp_sb = []
        for half in range(2):
            kp_half = sb.tile([P, 2, N], F32, name="kp%d" % half)
            nc.sync.dma_start(out=kp_half[:], in_=kp_rows[:, 2 * half : 2 * half + 2, :])
            kp_sb.extend([kp_half[:, 0, :], kp_half[:, 1, :]])
        y_sb = sb.tile([P, PACK, N], F32, name="y_sb")
        nc.sync.dma_start(out=y_sb[:], in_=y.rearrange("(p j) i -> p j i", j=PACK))

        window = []
        for t in range(PACK - 1):
            window.append(sb.tile([P, T], F32, name="window%d" % t))
            zero(window[t])

        x_by_d = sb.tile([P, PACK * R], BF16, name="x_by_d", align_bytes=64)
        dealt = x_by_d[:].rearrange("p (j s t) -> p j s t", j=PACK, t=PACK)
        x_cols = x_raw[:].rearrange("p t (s j) -> p j s t", j=PACK)
        nc.vector.tensor_copy(out=dealt[:, 0:3], in_=x_cols[:, 0:3])
        nc.scalar.copy(out=dealt[:, 3], in_=x_cols[:, 3])

        ts_col = {}
        for k, (name, lst) in enumerate((("old", old_list), ("new", new_list))):
            picked = sb.tile([P, N], F32, name="ts_picked_" + name)
            nc.vector.tensor_copy(out=picked[:], in_=ts_window[:].indirect(lst[:]))
            for q in range(PACK):
                cols = slice(q * P, (q + 1) * P)
                nc.tensor.transpose(bank[k][:, cols], picked[:, cols], ident[:])
            ts_col[name] = sb.tile([P, PACK], F32, name="ts_col_" + name)
        xq_d = quantize("xq_d", x_by_d, E4M3)
        for k, name in enumerate(("old", "new")):
            nc.vector.tensor_copy(out=ts_col[name][:], in_=bank[k][:, 0:N:P])
            for q in range(PACK):
                cols = slice(q * P, (q + 1) * P)
                nc.tensor.transpose(bank[4 + k][:, cols], ts_col[name][:, q : q + 1].to_broadcast([P, P]), ident[:])

        x_words = x_by_d[:].bitcast(F32).rearrange("p (j s u) -> p j s u", j=PACK, u=2)
        for u in range(2):
            for j in range(PACK):
                nc.tensor.transpose(bank[2 + u][:, j * P : (j + 1) * P], x_words[:, j, :, u], ident[:])

        w_pairs = [sb.tile([P, 2 * T], BF16, name="w_pairs%d" % u, tag="w_pairs%d" % u, align_bytes=64) for u in range(2)]
        w_new = sb.tile([P, PACK * N], BF16, name="w_new", align_bytes=64)
        w_old = sb.tile([P, PACK * N], BF16, name="w_old", tag="w_old", align_bytes=64)

        def cast_w(u, c0):
            dst = w_pairs[u][:, 2 * c0 : 2 * (c0 + W_CHUNK)].rearrange("p (c e) -> p c e", e=2)
            src = w_raw[u, c0][:].rearrange("p e c -> p c e")
            if u == 1 and c0 + W_CHUNK == T:
                nc.vector.tensor_copy(out=dst, in_=src)
            else:
                nc.scalar.activation(out=dst, in_=src, func=ACT.Copy)

        old_pairs = sb.tile([P, 2, N], U32, name="old_pairs", tag="old_pairs", align_bytes=64)
        new_words = w_new[:].bitcast(U32).rearrange("p (c u) -> p c u", u=2)

        def gather_w(dst, u, lst):
            nc.vector.tensor_copy(out=dst, in_=w_pairs[u][:].bitcast(U32).indirect(lst[:]))

        for c0 in range(0, T, W_CHUNK):
            cast_w(0, c0)
        gather_w(old_pairs[:, 0, :], 0, old_list)
        gather_w(new_words[:, :, 0], 0, new_list)

        us_half = sb.tile([P, PACK], F32, name="us_half")
        c1_half = sb.tile([P, PACK], F32, name="c1_half")
        c1_neg = sb.tile([P, PACK], F32, name="c1_neg")
        c2 = sb.tile([P, PACK], F32, name="c2")
        nc.vector.tensor_tensor(c2[:], row_vec["w2"][:], row_vec["us"][:], ALU.mult)
        nc.vector.tensor_scalar(us_half[:], row_vec["us"][:], 0.5, None, ALU.mult)
        nc.vector.scalar_tensor_tensor(c1_half[:], row_vec["w1"][:], 0.5, row_vec["us"][:], ALU.mult, ALU.mult)
        nc.vector.scalar_tensor_tensor(c1_neg[:], row_vec["w1"][:], -1.0, row_vec["us"][:], ALU.mult, ALU.mult)

        for c0 in range(0, T, W_CHUNK):
            cast_w(1, c0)
        gather_w(old_pairs[:, 1, :], 1, old_list)
        nc.vector.tensor_copy(
            out=w_old[:].bitcast(I32).rearrange("p (c u) -> p c u", u=2),
            in_=old_pairs[:].bitcast(I32).rearrange("p u c -> p c u"),
        )
        wq_old = quantize("wq_old", w_old, E4M3)
        new_upper = sb.tile([P, N], U32, name="new_upper", tag="w_old", align_bytes=64)
        gather_w(new_upper[:], 1, new_list)

        ts_row = {}

        def spread_ts(name, src, slot):
            ts_row[name] = sb.tile([P, N], F32, name="ts_row_" + name, tag=slot, align_bytes=64)
            nc.scalar.copy(out=ts_row[name][:], in_=src[:])

        spread_ts("old", bank[4], "w_raw1_1024")
        x_by_r = sb.tile([P, PACK * D], BF16, name="x_by_r", tag="w_raw1_1536", align_bytes=64)
        for u in range(2):
            nc.scalar.copy(
                out=x_by_r[:, u * 2 * D : (u + 1) * 2 * D].rearrange("s (e p j) -> s e p j", e=2, j=PACK),
                in_=bank[2 + u][:].bitcast(BF16).rearrange("s (j p e) -> s e p j", j=PACK, e=2),
            )
        spread_ts("new", bank[5], "old_pairs")
        nc.scalar.copy(out=new_words[:, :, 1], in_=new_upper[:])

        def add_turned(banks, src, j, first, last):
            for q in range(PACK):
                nc.tensor.matmul(
                    banks[q][:, j * P : (j + 1) * P],
                    src[:, q * P : (q + 1) * P],
                    ident[:],
                    start=first,
                    stop=last,
                    is_transpose=True,
                )

        def finish_gradient(name, banks, col, vector_helps):
            by_slot = sb.tile([P, PACK, R], BF16, name=name + "_by_slot")
            grad = sb.tile([P, PACK * N], BF16, name=name + "_by_r", tag=name + "_by_r", align_bytes=64)
            grad_words = grad[:].bitcast(F32)
            for q in range(PACK):
                dst = by_slot[:, q, :].rearrange("p (s j) -> p s j", j=PACK)
                src = banks[q][:].rearrange("p (j s) -> p s j", j=PACK)
                if vector_helps and q == PACK - 1:
                    nc.vector.tensor_scalar(dst, src, col[:, q : q + 1], None, ALU.mult)
                else:
                    nc.scalar.activation(out=dst, in_=src, func=ACT.Copy, scale=col[:, q : q + 1])
                if q % 2 == 1:
                    back = banks[q // 2]
                    for qq in (q - 1, q):
                        words = by_slot[:, qq, :].bitcast(F32).rearrange("p (s u) -> p s u", u=2)
                        for u in range(2):
                            place = 2 * (qq % 2) + u
                            nc.tensor.transpose(back[:, place * P : (place + 1) * P], words[:, :, u], ident[:])
            for half in range(2):
                nc.scalar.copy(
                    out=grad_words[:, half * N : (half + 1) * N].rearrange("s (q p u) -> s q p u", q=2, u=2),
                    in_=banks[half][:].rearrange("s (q u p) -> s q p u", q=2, u=2),
                )
            return quantize(name, grad, E5M2)

        h_banks = bank[4:8]
        neg_max = sb.tile([P, PACK], F32, name="neg_max", tag="neg_max", align_bytes=64)
        total = sb.tile([P, PACK], F32, name="total", tag="total")
        inverse = sb.tile([P, PACK], F32, name="inverse", tag="inverse", align_bytes=64)
        z = [sb.tile([P, N], F32, name="z%d" % j, tag="z%d" % j) for j in range(PACK)]

        def score(j):
            nc.vector.scalar_tensor_tensor(
                z[j][:], bank[j][:], row_vec["us"][:, j : j + 1], ts_row["old"][:], ALU.mult, ALU.mult
            )

        def exponentiate(j):
            col = slice(j, j + 1)
            nc.vector.tensor_reduce(neg_max[:, col], z[j][:], AX.X, ALU.max, negate=True)
            nc.scalar.activation(
                out=z[j][:], in_=z[j][:], func=ACT.Exp, bias=neg_max[:, col], accum_out=total[:, col]
            )

        def normalise(tiles):
            cols = slice(tiles[0], tiles[-1] + 1)
            nc.vector.reciprocal(inverse[:, cols], total[:, cols])
            for j in tiles:
                col = slice(j, j + 1)
                nc.vector.tensor_scalar(z[j][:], z[j][:], inverse[:, col], c2[:, col], ALU.mult, ALU.mult)
                add_turned(h_banks, z[j], j, False, j == PACK - 1)

        for j in range(PACK):
            product(bank[j], xq_d, j, wq_old)
        kept = sb.tile([P, PACK, N], F32, name="kept", tag="w_pairs1", align_bytes=64)
        for j in range(PACK):
            nc.gpsimd.tensor_scalar(kept[:, j, :], kp_sb[j], c2[:, j : j + 1], -1.0, ALU.mult, ALU.mult)
            add_turned(h_banks, kept[:, j, :], j, j == 0, False)
        for step in range(PACK + 1):
            if step < PACK:
                score(step)
            if step >= 1:
                exponentiate(step - 1)
        normalise([0, 1, 2])
        normalise([3])
        xq_r = quantize("xq_r", x_by_r, E4M3, "inverse")
        hq = finish_gradient("h", h_banks, ts_col["old"], True)

        wq_new = quantize("wq_new", w_new, E4M3, "neg_max")
        window.append(sb.tile([P, T], F32, name="window3", tag="total"))
        zero(window[3])
        act = []
        for j in range(PACK):
            product(bank[j], xq_d, j, wq_new)
            act.append(sb.tile([P, N], F32, name="a%d" % j))
            nc.vector.tensor_tensor(act[j][:], bank[j][:], ts_row["new"][:], ALU.mult)

        def stage(name, acc, copy, slot):
            staged = sb.tile([P, N], F32, name=name, tag=slot, align_bytes=64)
            copy(out=staged[:], in_=acc[:])
            return staged

        def scatter(t, lst, staged):
            nc.vector.tensor_copy(out=window[t][:].indirect(lst[:]), in_=staged[:])

        d2_banks = bank[6:8] + bank[4:6]
        for t in range(PACK):
            product(d2_banks[t], xq_r, t, hq)
        for t in range(PACK - 1):
            scatter(t, old_list, stage("d2_%d" % t, d2_banks[t], nc.scalar.copy, "d2_%d" % t))

        g_banks = bank[0:4]
        target = sb.tile([P, PACK, N], F32, name="target", tag="z3")
        for j in range(PACK):
            nc.gpsimd.tensor_scalar(target[:, j, :], y_sb[:, j, :], -0.5, c1_neg[:, j : j + 1], ALU.add, ALU.mult)
            add_turned(g_banks, target[:, j, :], j, j == 0, False)
        for j in range(PACK):
            col = slice(j, j + 1)
            nc.scalar.activation(out=act[j][:], in_=act[j][:], func=ACT.Tanh, scale=us_half[:, col])
            nc.scalar.activation(out=act[j][:], in_=act[j][:], func=ACT.Copy, scale=c1_half[:, col])
            add_turned(g_banks, act[j], j, False, j == PACK - 1)
        gq = finish_gradient("g", g_banks, ts_col["new"], False)
        scatter(3, old_list, stage("d2_3", d2_banks[3], nc.vector.tensor_copy, "g_by_r"))

        out_rows = out.rearrange("(p t) c -> p t c", t=PACK)
        d1_banks = bank[6:8] + bank[4:5] + bank[2:3]
        for t in range(PACK):
            product(d1_banks[t], xq_r, t, gq)
            scatter(t, new_list, stage("d1_%d" % t, d1_banks[t], nc.scalar.copy, "d1_%d" % t))
            nc.sync.dma_start(out=out_rows[:, t, :], in_=window[t][:])
